import numpy as np, ml_dtypes
CORES = [7,39,87,119,135,167,215,247,263,295,343,375,391,423,471,503]
N = 16
TK = 128
COEF = [[2,-1,0,0,0,0,0,0,1,0,0,0,0,0,0,-1],[-1,2,-1,0,0,0,0,0,0,1,0,0,0,0,0,0],[0,-1,2,-1,0,0,0,0,0,0,1,0,0,0,0,0],[0,0,-1,2,-1,0,0,0,0,0,0,1,0,0,0,0],[0,0,0,-1,2,-1,0,0,0,0,0,0,1,0,0,0],[0,0,0,0,-1,2,-1,0,0,0,0,0,0,1,0,0],[0,0,0,0,0,-1,2,-1,0,0,0,0,0,0,1,0],[0,0,0,0,0,0,-1,2,-1,0,0,0,0,0,0,1],[1,0,0,0,0,0,0,-1,2,-1,0,0,0,0,0,0],[0,1,0,0,0,0,0,0,-1,2,-1,0,0,0,0,0],[0,0,1,0,0,0,0,0,0,-1,2,-1,0,0,0,0],[0,0,0,1,0,0,0,0,0,0,-1,2,-1,0,0,0],[0,0,0,0,1,0,0,0,0,0,0,-1,2,-1,0,0],[0,0,0,0,0,1,0,0,0,0,0,0,-1,2,-1,0],[0,0,0,0,0,0,1,0,0,0,0,0,0,-1,2,-1],[-1,0,0,0,0,0,0,1,0,0,0,0,0,0,-1,2]]
def setup_inputs(rng):
    return {"x": rng.standard_normal((N, 128, TK), dtype=np.float32).astype(ml_dtypes.bfloat16), "a": (rng.standard_normal((N, 128, 128), dtype=np.float32) / 11).astype(ml_dtypes.bfloat16)}
def setup_inputs_big(rng):
    d = setup_inputs(rng)
    for k in ("x", "a"): d[k] = (d[k].astype(np.float32) * 1024.0).astype(d[k].dtype)
    return d
def setup_inputs_small(rng):
    d = setup_inputs(rng)
    for k in ("x", "a"): d[k] = (d[k].astype(np.float32) * (1 / 1024.0)).astype(d[k].dtype)
    return d
def setup_inputs_apart(rng):
    d = setup_inputs(rng)
    f = (10.0 ** rng.permutation(np.linspace(-1.5, 1.5, N))).astype(np.float32).reshape(N, 1, 1)
    for k in ("x", "a"): d[k] = (d[k].astype(np.float32) * f).astype(d[k].dtype)
    return d
def reference(x, a):
    X, A = x.astype(np.float64), a.astype(np.float64)
    y = np.stack([A[r].T @ sum(COEF[r][j] * X[j] for j in range(N)) for r in range(N)])
    return {"y": y.astype(ml_dtypes.bfloat16)}

from concourse.bass import DstId, RemoteDMATransfer
from concourse.mybir import AluOpType

W = 128
NSLOT = 3
NWEIGHT = 2

SCRATCH = {
    "xd": ("dram", [128, W], "bfloat16"),
    "rd": ("dram", [128, W], "bfloat16"),
    "xs": ("sbuf", [128, W], "bfloat16"),
    "a1": ("sbuf", [128, W], "bfloat16"),
    "cw": ("sbuf", [128, NWEIGHT * W], "bfloat16"),
    "aw": ("sbuf", [128, NWEIGHT * W], "bfloat16"),
    "land": ("sbuf", [128, NSLOT * W], "bfloat16"),
    "ps": ("psum", [128, W], "float32"),
    "ys": ("sbuf", [128, W], "bfloat16"),
}
SEMAPHORES = ["ldx", "lda", "lds", "go", "fill", "wrdy", "rarr", "narr", "darr", "sent", "mm", "cp", "stored"]


def _engines(mask):
    return [k for k in range(16) if (mask >> k) & 1]


def _bits(engines):
    m = 0
    for k in engines:
        m |= 1 << k
    return m


def _plan(T, topo):
    cores, coef = T.cores, T.tables["COEF"]
    n = len(cores)
    need = [[j for j in range(n) if j != r and coef[r][j] != 0] for r in range(n)]
    via = {}
    for r in range(n):
        for j in need[r]:
            s, d = cores[j], cores[r]
            if topo.may_write(s, d):
                via[(j, r)] = None
                continue
            cand = [q for q in range(n) if q != j and q != r
                    and topo.may_write(s, cores[q]) and topo.may_write(cores[q], d)]
            good = [q for q in cand
                    if topo.rack(topo.host(cores[q])) != topo.rack(topo.host(s))
                    and topo.chip(cores[q]) == topo.chip(s) and topo.same_plane(cores[q], d)]
            via[(j, r)] = (good or cand)[0]
    return need, via


def rank_program(g, core, T, topo):
    me = T.rank_of(core)
    if me is None:
        return
    cores, coef = T.cores, T.tables["COEF"]
    n = len(cores)
    need, via = _plan(T, topo)
    S = T.sem

    def slot(r, j):
        k = need[r].index(j)
        return T.land[:, k * W:(k + 1) * W]

    direct_out = [r for r in range(n) if me in need[r] and via[(me, r)] is None]
    relay_out = [r for r in range(n) if me in need[r] and via[(me, r)] is not None]
    forward = [(j, r) for (j, r), q in sorted(via.items()) if q == me]
    direct_in = [j for j in need[me] if via[(j, me)] is None]
    relay_in = [j for j in need[me] if via[(j, me)] is not None]
    assert len(need[me]) <= NSLOT and len(forward) <= 1 and len(relay_out) <= 1

    def first_mask(src, dst):
        e = _engines(topo.mask(src, dst))
        return e[:len(e) // 2]

    def full_mask(src, dsts):
        m = topo.mask(src, dsts[0])
        for d in dsts[1:]:
            m &= topo.mask(src, d)
        return _engines(m)

    g.sync.dma_start(T.xd[:], T.x[:]).then_inc(S.ldx, 16)
    g.sync.sem_inc(S.go, 1)
    g.sync.dma_start(T.xs[:], T.x[:]).then_inc(S.lds, 16)
    g.scalar.wait_ge(S.go, 1)
    g.scalar.dma_start(T.a1[:], T.a[:]).then_inc(S.lda, 16)

    weights = sorted(set(coef[me][j] for j in need[me] + [me]) - {1})
    assert len(weights) <= NWEIGHT
    for k, w in enumerate(weights):
        g.vector.memset(T.cw[:, k * W:(k + 1) * W], float(w)).then_inc(S.fill, 1)
    if weights:
        g.vector.wait_ge(S.fill, len(weights))
        g.vector.wait_ge(S.lda, 16)
    for k, w in enumerate(weights):
        c = slice(k * W, (k + 1) * W)
        g.vector.tensor_tensor(T.aw[:, c], T.a1[:], T.cw[:, c], AluOpType.mult).then_inc(S.wrdy, 1)

    def lhs(j):
        w = coef[me][j]
        if w == 1:
            return T.a1[:]
        k = weights.index(w)
        return T.aw[:, k * W:(k + 1) * W]

    sent = 0
    g.wait_ge(S.ldx, 16)
    for r in relay_out:
        q = cores[via[(me, r)]]
        e = first_mask(core, q)
        rid, pid = topo.addr(q, core)
        g.remote_dma(T.rd[:], T.xd[:], S.rarr, S.sent, pid, rid, _bits(e))
        sent += len(e)
    if direct_out:
        dst = [cores[r] for r in direct_out]
        e = full_mask(core, dst)
        ids = []
        for d in dst:
            rid, pid = topo.addr(d, core)
            ids.append(DstId(rid=rid, pnc=pid))
        g.remote_dma_fused([RemoteDMATransfer(dst_ids=ids, dma_engine_mask=_bits(e), remote_sem=S.narr,
                                              srcs=[T.xd[:]], dsts=[slot(r, me) for r in direct_out], alu_op=0)],
                           local_sem=S.sent)
        sent += len(e)
    for (j, r) in forward:
        g.wait_ge(S.rarr, len(first_mask(cores[j], core)))
        e = full_mask(core, [cores[r]])
        rid, pid = topo.addr(cores[r], core)
        g.remote_dma(slot(r, j), T.rd[:], S.darr, S.sent, pid, rid, _bits(e))
        sent += len(e)

    order = [me] + direct_in + relay_in
    g.tensor.wait_ge(S.lda, 16)
    g.tensor.wait_ge(S.lds, 16)
    if weights:
        g.tensor.wait_ge(S.wrdy, len(weights))
    for i, j in enumerate(order):
        if direct_in and j == direct_in[0]:
            g.tensor.wait_ge(S.narr, sum(len(full_mask(cores[s], [cores[r] for r in range(n)
                                                                  if s in need[r] and via[(s, r)] is None]))
                                         for s in direct_in))
        if relay_in and j == relay_in[0]:
            g.tensor.wait_ge(S.darr, sum(len(full_mask(cores[via[(s, me)]], [core])) for s in relay_in))
        rhs = T.xs[:] if j == me else slot(me, j)
        mmi = g.tensor.matmul(T.ps[:], lhs(j), rhs, i == 0, i == len(order) - 1)
        if i == len(order) - 1:
            mmi.then_inc(S.mm, 1)

    g.vector.wait_ge(S.mm, 1)
    g.vector.tensor_copy(T.ys[:], T.ps[:]).then_inc(S.cp, 1)
    g.sync.wait_ge(S.cp, 1)
    g.sync.dma_start(T.y[:], T.ys[:]).then_inc(S.stored, 16)
    g.sync.wait_ge(S.stored, 16)
    if sent:
        g.wait_ge(S.sent, sent)
